import numpy as np
import ml_dtypes


def mxq(x, axis, fmt="e4m3"):
    dtype, down = {"e4m3": (ml_dtypes.float8_e4m3fn, 7), "e5m2": (ml_dtypes.float8_e5m2, 14)}[fmt]
    v = np.moveaxis(np.asarray(x, np.float32).astype(ml_dtypes.bfloat16).astype(np.float64), axis, -1)
    blocks = v.reshape(v.shape[:-1] + (-1, 32))
    amax = np.abs(blocks).max(-1, keepdims=True)
    byte = np.maximum(np.where(amax > 0, np.frexp(amax)[1] - 1 + 127, 0) - down, 1)
    scale = np.exp2(byte - 127.0)
    codes = (blocks / scale).astype(np.float32).astype(dtype).astype(np.float64)
    return np.moveaxis((codes * scale).reshape(v.shape), -1, axis)


WIDE = False


def mx_kscale(k):
    if not WIDE:
        return np.ones(k)
    levels = np.array([10, -10, 5, -5, 0])
    if k % 512:
        return np.exp2(np.random.permutation(np.resize(levels, k // 32))).repeat(32)
    a = np.empty((k // 512, 16))
    for p in range(k // 512):
        a[p, :8] = np.random.permutation(np.resize(levels, 8))
        for g in range(8):
            far = levels[np.abs(levels - a[p, g]) >= 10]
            a[p, g + 8] = far[np.random.randint(len(far))]
    return np.exp2(a.ravel()).repeat(32)


def f64(x):
    return np.asarray(x).astype(np.float64)


def striped(idx):
    return np.tile(idx.reshape(-1, 16).T, (8, 1)).astype(np.uint16)


def unstriped(offs):
    return offs[:16].T.reshape(-1).astype(np.int64)


def pack_weight(w):
    k, n = w.shape
    w = f64(np.asarray(w, np.float32).astype(ml_dtypes.bfloat16)).reshape(k // 32, 32, n)
    amax = np.abs(w).max(1)
    byte = np.clip(np.where(amax > 0, np.frexp(amax)[1] - 1 + 127 - 7, 1), 1, 254)
    scaled = (w * np.exp2(127.0 - byte)[:, None, :]).reshape(k, n).astype(np.float32)
    words = np.ascontiguousarray(scaled.reshape(k // 512, 128, 4, n).transpose(0, 1, 3, 2)).astype(ml_dtypes.float8_e4m3fn).view(np.uint8)
    return words, np.ascontiguousarray(byte.astype(np.uint8).reshape(k // 512, 16, n))


def unpack_weight(words, scales):
    g, p, n, _ = words.shape
    vals = np.ascontiguousarray(words).view(ml_dtypes.float8_e4m3fn).astype(np.float64) * np.repeat(np.exp2(scales.astype(np.float64) - 127.0), 8, axis=1)[..., None]
    return vals.transpose(0, 1, 3, 2).reshape(g * 512, n)


def sigmoid(v):
    return 1.0 / (1.0 + np.exp(-np.maximum(v, -700.0)))


K, T, S, N = 1024, 1024, 512, 256
P = 2 ** 7


def setup_inputs():
    n = np.random.standard_normal
    s = mx_kscale(K)[:, None]
    packed_xT = pack_weight(n((K, T)) * s)
    return {
        "x_words": packed_xT[0],
        "x_scales": packed_xT[1],
        "w1": (n((K, N)) / np.sqrt(K) / s).astype(np.float32),
        "w2": (n((K, N)) / np.sqrt(K) / s).astype(np.float32),
        "w3": (n((K, N)) / np.sqrt(K) / s).astype(np.float32),
        "imp": (np.tile(np.random.uniform(0.5, 1.5, S), (P, 1))).astype(np.float32),
        "offs": striped(np.random.permutation(T)[:S]),
    }


def reference(x_words, x_scales, w1, w2, w3, imp, offs):
    xq = unpack_weight(x_words, x_scales)[:, unstriped(offs)]
    yb = mxq(f64(w1), 0, "e4m3").T @ xq
    yc = mxq(f64(w2), 0, "e4m3").T @ xq
    yg = mxq(f64(w3), 0, "e4m3").T @ xq
    lone = (yb * yc) * sigmoid(yg) + yb
    l2 = (lone) ** 2
    ms = l2.mean(axis=1, keepdims=True)
    return (lone / np.sqrt(ms + 0.1)) * f64(imp)[:1]

@@ -1,0 +1,158 @@
+from contextlib import ExitStack
+
+import concourse.mybir as mybir
+
+K, T, S, N = 1024, 1024, 512, 256
+P = 128
+PACK = 4
+K_PASS = P * PACK
+PASSES = K // K_PASS
+HALF = S // 2
+FLOPS = 3 * 2 * K * N * S
+
+F32 = mybir.dt.float32
+BF16 = mybir.dt.bfloat16
+I32 = mybir.dt.int32
+U32 = mybir.dt.uint32
+U16 = mybir.dt.uint16
+U8 = mybir.dt.uint8
+FP8X4 = mybir.dt.float8_e4m3fn_x4
+ACT = mybir.ActivationFunctionType
+ALU = mybir.AluOpType
+
+
+def tile_picked_ygatcr_rms_p_kernel(tc, x_words, x_scales, w1, w2, w3, imp, offs, out):
+    nc = tc.nc
+    with ExitStack() as ctx:
+        keep = ctx.enter_context(tc.tile_pool(name="keep", bufs=1))
+        psum = ctx.enter_context(tc.psum_pool(name="psum", bufs=1))
+
+        offsets = keep.tile([P, S // 16], U16, name="offsets")
+        scale_table = keep.tile([P, T], U8, name="scale_table", align_bytes=64)
+        nc.vector.memset(scale_table[:].bitcast(I32), 0)
+        minus_half = keep.tile([P, 1], F32, name="minus_half")
+        nc.gpsimd.memset(minus_half[:], -0.5)
+
+        def load_x(o):
+            table = keep.tile([P, T], I32, name="word_table%d" % o, align_bytes=64)
+            nc.sync.dma_start(table[:], x_words[o].rearrange("p c r -> p (c r)").bitcast(I32))
+            return table
+
+        def load_w(w, o, c0, width, name):
+            raw = keep.tile([P, PACK, width], F32, name="raw_" + name, align_bytes=64)
+            rows = w[o * K_PASS : (o + 1) * K_PASS, c0 : c0 + width]
+            nc.sync.dma_start(raw[:], rows.rearrange("(p t) m -> p t m", t=PACK))
+            return raw
+
+        raw_g0 = load_w(w3, 0, 0, N, "g0")
+        nc.sync.dma_start(offsets[:], offs)
+        for q in range(4):
+            nc.sync.dma_start(
+                scale_table[32 * q : 32 * q + 8, :].bitcast(I32),
+                x_scales[:, 4 * q : 4 * q + 4, :].bitcast(I32),
+            )
+        table0 = load_x(0)
+        raw_g1 = load_w(w3, 1, 0, N, "g1")
+        table1 = load_x(1)
+        raw_c0 = load_w(w2, 0, 0, N, "c0")
+        raw_c1 = load_w(w2, 1, 0, N, "c1")
+        raw_b0 = load_w(w1, 0, 0, N, "b0")
+        raw_b10 = load_w(w1, 1, 0, P, "b10")
+        raw_b11 = load_w(w1, 1, P, P, "b11")
+        imp_sb = keep.tile([P, S], F32, name="imp_sb", align_bytes=64)
+        nc.sync.dma_start(imp_sb[:], imp)
+
+        def interleave(raw, width, on_scalar, name):
+            grouped = keep.tile([P, width * PACK], BF16, name="grouped_" + name, align_bytes=64)
+            for copy, a, b in ((nc.scalar.copy, 0, on_scalar), (nc.vector.tensor_copy, on_scalar, width)):
+                if b > a:
+                    copy(
+                        grouped[:, a * PACK : b * PACK].rearrange("p (c i t) -> p c t i", i=4, t=PACK),
+                        raw[:, :, a:b].rearrange("p t (c i) -> p c t i", i=4),
+                    )
+            return grouped
+
+        def quantize(grouped, width, name):
+            codes = keep.tile([P, width], U32, name="codes_" + name, align_bytes=64)
+            scales = keep.tile([P, width], U8, name="scales_" + name, align_bytes=64)
+            nc.vector.quantize_mx(out=codes[:].bitcast(FP8X4), scales=scales[:], in_=grouped[:])
+            return codes, scales
+
+        picked_scales = keep.tile([P, S], U8, name="picked_scales", align_bytes=64)
+        picked = [keep.tile([P, S], U32, name="picked%d" % o, align_bytes=64) for o in range(PASSES)]
+
+        def product(bank, wq, c0, o, j0, width):
+            codes, scales = wq
+            nc.tensor.matmul_mx(
+                out=bank[:],
+                lhsT=codes[:, c0 : c0 + P].bitcast(FP8X4),
+                lhsT_scale=scales[:, c0 : c0 + P],
+                rhs=picked[o][:, j0 : j0 + width].bitcast(FP8X4),
+                rhs_scale=picked_scales[4 * o : P, j0 : j0 + width],
+                start=(o == 0),
+                stop=(o == PASSES - 1),
+            )
+
+        yg = [psum.tile([P, S], F32, name="yg%d" % m) for m in range(2)]
+        yc = [psum.tile([P, S], F32, name="yc%d" % m) for m in range(2)]
+        yb = [[psum.tile([P, HALF], F32, name="yb%d%d" % (m, h)) for h in range(2)] for m in range(2)]
+
+        nc.vector.tensor_copy(picked_scales[:], scale_table[:].indirect(offsets[:]))
+        gr = interleave(raw_g0, N, N, "g0")
+        nc.vector.tensor_copy(picked[0][:], table0[:].bitcast(U32).indirect(offsets[:]))
+        q_g0 = quantize(gr, N, "g0")
+        for m in range(2):
+            product(yg[m], q_g0, m * P, 0, 0, S)
+        gr = interleave(raw_g1, N, N, "g1")
+        nc.vector.tensor_copy(picked[1][:], table1[:].bitcast(U32).indirect(offsets[:]))
+        q_g1 = quantize(gr, N, "g1")
+        for m in range(2):
+            product(yg[m], q_g1, m * P, 1, 0, S)
+        gr = interleave(raw_c0, N, N, "c0")
+        q_c0 = quantize(gr, N, "c0")
+        for m in range(2):
+            product(yc[m], q_c0, m * P, 0, 0, S)
+        th = []
+        for m in range(2):
+            t = keep.tile([P, S], F32, name="th%d" % m, align_bytes=64)
+            nc.scalar.activation(t[:], yg[m][:], ACT.Tanh, scale=0.5)
+            th.append(t)
+        gr = interleave(raw_c1, N, P, "c1")
+        q_c1 = quantize(gr, N, "c1")
+        for m in range(2):
+            product(yc[m], q_c1, m * P, 1, 0, S)
+        gr = interleave(raw_b0, N, N, "b0")
+        gated = []
+        for m in range(2):
+            a = keep.tile([P, S], F32, name="gated%d" % m, align_bytes=64)
+            nc.vector.scalar_tensor_tensor(a[:], th[m][:], 1.0, yc[m][:], ALU.add, ALU.mult)
+            gated.append(a)
+        q_b0 = quantize(gr, N, "b0")
+        for m in range(2):
+            for h in range(2):
+                product(yb[m][h], q_b0, m * P, 0, h * HALF, HALF)
+        for m, raw in enumerate((raw_b10, raw_b11)):
+            gr = interleave(raw, P, 64, "b1%d" % m)
+            q = quantize(gr, P, "b1%d" % m)
+            for h in range(2):
+                product(yb[m][h], q, 0, 1, h * HALF, HALF)
+        lone = [keep.tile([P, S], F32, name="lone%d" % m, align_bytes=64) for m in range(2)]
+        rstd = []
+        for m in range(2):
+            sums = keep.tile([P, 2], F32, name="sums%d" % m)
+            squares = keep.tile([P, S], F32, name="squares%d" % m, align_bytes=64)
+            for h in range(2):
+                cols = slice(h * HALF, (h + 1) * HALF)
+                nc.vector.scalar_tensor_tensor(lone[m][:, cols], gated[m][:, cols], 2.0, yb[m][h][:], ALU.add, ALU.mult)
+                nc.scalar.activation(squares[:, cols], lone[m][:, cols], ACT.Square, scale=S**-0.5, accum_out=sums[:, h : h + 1])
+            total = keep.tile([P, 1], F32, name="total%d" % m)
+            nc.vector.tensor_scalar(total[:], sums[:, 0:1], sums[:, 1:2], 0.4, ALU.add, ALU.add)
+            r = keep.tile([P, 1], F32, name="rstd%d" % m)
+            nc.gpsimd.tensor_tensor(r[:], total[:], minus_half[:], ALU.pow)
+            rstd.append(r)
+        for m in range(2):
+            res = keep.tile([P, S], F32, name="res%d" % m, align_bytes=64)
+            for h in range(2):
+                cols = slice(h * HALF, (h + 1) * HALF)
+                nc.vector.scalar_tensor_tensor(res[:, cols], lone[m][:, cols], rstd[m][:], imp_sb[:, cols], ALU.mult, ALU.mult)
+                nc.sync.dma_start(out[m * P : (m + 1) * P, cols], res[:, cols])

@@ -27,132 +27,142 @@ def tile_picked_ygatcr_rms_p_kernel(tc, x_words, x_scales, w1, w2, w3, imp, offs
         keep = ctx.enter_context(tc.tile_pool(name="keep", bufs=1))
         psum = ctx.enter_context(tc.psum_pool(name="psum", bufs=1))
 
+        def tile(shape, dtype, name, tag=None):
+            return keep.tile(shape, dtype, name=name, tag=tag or name, align_bytes=64)
+
         offsets = keep.tile([P, S // 16], U16, name="offsets")
-        scale_table = keep.tile([P, T], U8, name="scale_table", align_bytes=64)
-        nc.vector.memset(scale_table[:].bitcast(I32), 0)
-        minus_half = keep.tile([P, 1], F32, name="minus_half")
+        scale_table = tile([P, T], U8, "scale_table")
+        nc.gpsimd.memset(scale_table[:].bitcast(I32), 0)
+        minus_half = tile([P, 1], F32, "minus_half")
         nc.gpsimd.memset(minus_half[:], -0.5)
+        lone = {}
+
+        word_table = [tile([P, T], I32, "word_table%d" % o) for o in range(PASSES)]
 
         def load_x(o):
-            table = keep.tile([P, T], I32, name="word_table%d" % o, align_bytes=64)
-            nc.sync.dma_start(table[:], x_words[o].rearrange("p c r -> p (c r)").bitcast(I32))
-            return table
+            nc.sync.dma_start(word_table[o][:], x_words[o].rearrange("p c r -> p (c r)").bitcast(I32))
 
-        def load_w(w, o, c0, width, name):
-            raw = keep.tile([P, PACK, width], F32, name="raw_" + name, align_bytes=64)
-            rows = w[o * K_PASS : (o + 1) * K_PASS, c0 : c0 + width]
-            nc.sync.dma_start(raw[:], rows.rearrange("(p t) m -> p t m", t=PACK))
-            return raw
+        raw = {}
 
-        raw_g0 = load_w(w3, 0, 0, N, "g0")
+        def load_w(name, w, m, passes=range(PASSES)):
+            for o in passes:
+                raw[name, m, o] = tile([P, K_PASS], F32, "raw_%s%d%d" % (name, m, o))
+                rows = w[o * K_PASS : (o + 1) * K_PASS, m * P : (m + 1) * P]
+                nc.sync.dma_start(
+                    raw[name, m, o][:].rearrange("p (t m) -> p t m", t=PACK),
+                    rows.rearrange("(p t) m -> p t m", t=PACK),
+                )
+
+        load_w("g", w3, 0, [0])
         nc.sync.dma_start(offsets[:], offs)
         for q in range(4):
             nc.sync.dma_start(
                 scale_table[32 * q : 32 * q + 8, :].bitcast(I32),
                 x_scales[:, 4 * q : 4 * q + 4, :].bitcast(I32),
             )
-        table0 = load_x(0)
-        raw_g1 = load_w(w3, 1, 0, N, "g1")
-        table1 = load_x(1)
-        raw_c0 = load_w(w2, 0, 0, N, "c0")
-        raw_c1 = load_w(w2, 1, 0, N, "c1")
-        raw_b0 = load_w(w1, 0, 0, N, "b0")
-        raw_b10 = load_w(w1, 1, 0, P, "b10")
-        raw_b11 = load_w(w1, 1, P, P, "b11")
-        imp_sb = keep.tile([P, S], F32, name="imp_sb", align_bytes=64)
+        load_x(0)
+        load_w("g", w3, 0, [1])
+        load_x(1)
+        load_w("c", w2, 0)
+        load_w("g", w3, 1)
+        load_w("c", w2, 1)
+        load_w("b", w1, 0)
+        load_w("b", w1, 1)
+        imp_sb = tile([P, S], F32, "imp_sb")
         nc.sync.dma_start(imp_sb[:], imp)
 
-        def interleave(raw, width, on_scalar, name):
-            grouped = keep.tile([P, width * PACK], BF16, name="grouped_" + name, align_bytes=64)
-            for copy, a, b in ((nc.scalar.copy, 0, on_scalar), (nc.vector.tensor_copy, on_scalar, width)):
-                if b > a:
-                    copy(
-                        grouped[:, a * PACK : b * PACK].rearrange("p (c i t) -> p c t i", i=4, t=PACK),
-                        raw[:, :, a:b].rearrange("p t (c i) -> p c t i", i=4),
-                    )
-            return grouped
+        picked_scales = tile([P, S], U8, "picked_scales")
+        picked = [tile([P, S], U32, "picked0")]
+        nc.vector.tensor_copy(picked_scales[:], scale_table[:].indirect(offsets[:]))
+        nc.vector.tensor_copy(picked[0][:], word_table[0][:].bitcast(U32).indirect(offsets[:]))
+
+        def interleave(copy, dst, src):
+            copy(dst.rearrange("p (c i t) -> p c t i", i=4, t=PACK), src.rearrange("p (t c i) -> p c t i", i=4, t=PACK))
 
         def quantize(grouped, width, name):
-            codes = keep.tile([P, width], U32, name="codes_" + name, align_bytes=64)
-            scales = keep.tile([P, width], U8, name="scales_" + name, align_bytes=64)
-            nc.vector.quantize_mx(out=codes[:].bitcast(FP8X4), scales=scales[:], in_=grouped[:])
+            codes = tile([P, width], U32, "codes_" + name)
+            scales = tile([P, width], U8, "scales_" + name)
+            nc.vector.quantize_mx(out=codes[:].bitcast(FP8X4), scales=scales[:], in_=grouped)
             return codes, scales
 
-        picked_scales = keep.tile([P, S], U8, name="picked_scales", align_bytes=64)
-        picked = [keep.tile([P, S], U32, name="picked%d" % o, align_bytes=64) for o in range(PASSES)]
-
-        def product(bank, wq, c0, o, j0, width):
-            codes, scales = wq
+        def mx_pass(bank, codes, scales, o):
             nc.tensor.matmul_mx(
                 out=bank[:],
-                lhsT=codes[:, c0 : c0 + P].bitcast(FP8X4),
-                lhsT_scale=scales[:, c0 : c0 + P],
-                rhs=picked[o][:, j0 : j0 + width].bitcast(FP8X4),
-                rhs_scale=picked_scales[4 * o : P, j0 : j0 + width],
+                lhsT=codes.bitcast(FP8X4),
+                lhsT_scale=scales,
+                rhs=picked[o][:].bitcast(FP8X4),
+                rhs_scale=picked_scales[4 * o : P, :],
                 start=(o == 0),
                 stop=(o == PASSES - 1),
             )
 
-        yg = [psum.tile([P, S], F32, name="yg%d" % m) for m in range(2)]
-        yc = [psum.tile([P, S], F32, name="yc%d" % m) for m in range(2)]
-        yb = [[psum.tile([P, HALF], F32, name="yb%d%d" % (m, h)) for h in range(2)] for m in range(2)]
+        on_v, on_s = nc.vector.tensor_copy, nc.scalar.copy
+        grouped = {}
 
-        nc.vector.tensor_copy(picked_scales[:], scale_table[:].indirect(offsets[:]))
-        gr = interleave(raw_g0, N, N, "g0")
-        nc.vector.tensor_copy(picked[0][:], table0[:].bitcast(U32).indirect(offsets[:]))
-        q_g0 = quantize(gr, N, "g0")
-        for m in range(2):
-            product(yg[m], q_g0, m * P, 0, 0, S)
-        gr = interleave(raw_g1, N, N, "g1")
-        nc.vector.tensor_copy(picked[1][:], table1[:].bitcast(U32).indirect(offsets[:]))
-        q_g1 = quantize(gr, N, "g1")
-        for m in range(2):
-            product(yg[m], q_g1, m * P, 1, 0, S)
-        gr = interleave(raw_c0, N, N, "c0")
-        q_c0 = quantize(gr, N, "c0")
-        for m in range(2):
-            product(yc[m], q_c0, m * P, 0, 0, S)
-        th = []
-        for m in range(2):
-            t = keep.tile([P, S], F32, name="th%d" % m, align_bytes=64)
-            nc.scalar.activation(t[:], yg[m][:], ACT.Tanh, scale=0.5)
-            th.append(t)
-        gr = interleave(raw_c1, N, P, "c1")
-        q_c1 = quantize(gr, N, "c1")
-        for m in range(2):
-            product(yc[m], q_c1, m * P, 1, 0, S)
-        gr = interleave(raw_b0, N, N, "b0")
-        gated = []
-        for m in range(2):
-            a = keep.tile([P, S], F32, name="gated%d" % m, align_bytes=64)
-            nc.vector.scalar_tensor_tensor(a[:], th[m][:], 1.0, yc[m][:], ALU.add, ALU.mult)
-            gated.append(a)
-        q_b0 = quantize(gr, N, "b0")
-        for m in range(2):
-            for h in range(2):
-                product(yb[m][h], q_b0, m * P, 0, h * HALF, HALF)
-        for m, raw in enumerate((raw_b10, raw_b11)):
-            gr = interleave(raw, P, 64, "b1%d" % m)
-            q = quantize(gr, P, "b1%d" % m)
-            for h in range(2):
-                product(yb[m][h], q, 0, 1, h * HALF, HALF)
-        lone = [keep.tile([P, S], F32, name="lone%d" % m, align_bytes=64) for m in range(2)]
-        rstd = []
-        for m in range(2):
-            sums = keep.tile([P, 2], F32, name="sums%d" % m)
-            squares = keep.tile([P, S], F32, name="squares%d" % m, align_bytes=64)
-            for h in range(2):
-                cols = slice(h * HALF, (h + 1) * HALF)
-                nc.vector.scalar_tensor_tensor(lone[m][:, cols], gated[m][:, cols], 2.0, yb[m][h][:], ALU.add, ALU.mult)
-                nc.scalar.activation(squares[:, cols], lone[m][:, cols], ACT.Square, scale=S**-0.5, accum_out=sums[:, h : h + 1])
-            total = keep.tile([P, 1], F32, name="total%d" % m)
-            nc.vector.tensor_scalar(total[:], sums[:, 0:1], sums[:, 1:2], 0.4, ALU.add, ALU.add)
-            r = keep.tile([P, 1], F32, name="rstd%d" % m)
-            nc.gpsimd.tensor_tensor(r[:], total[:], minus_half[:], ALU.pow)
-            rstd.append(r)
-        for m in range(2):
-            res = keep.tile([P, S], F32, name="res%d" % m, align_bytes=64)
-            for h in range(2):
-                cols = slice(h * HALF, (h + 1) * HALF)
-                nc.vector.scalar_tensor_tensor(res[:, cols], lone[m][:, cols], rstd[m][:], imp_sb[:, cols], ALU.mult, ALU.mult)
+        def cast(name, m, first_copy, second_copy):
+            grouped[name, m] = tile([P, PASSES * K_PASS], BF16, "grouped_%s%d" % (name, m))
+            interleave(first_copy, grouped[name, m][:, :K_PASS], raw[name, m, 0][:])
+            interleave(second_copy, grouped[name, m][:, K_PASS:], raw[name, m, 1][:])
+
+        def both_passes(name, m, codes, scales):
+            bank = psum.tile([P, S], F32, name="y_%s%d" % (name, m))
+            for o in range(PASSES):
+                mx_pass(bank, codes[:, o * P : (o + 1) * P], scales[:, o * P : (o + 1) * P], o)
+            return bank
+
+        def product(name, m):
+            return both_passes(name, m, *quantize(grouped[name, m][:], PASSES * P, "%s%d" % (name, m)))
+
+        def gate(th, yg):
+            nc.scalar.activation(th[:], yg[:], ACT.Tanh, scale=0.5)
+            return th
+
+        def cross(m, th, yc, tag=None):
+            gated = tile([P, S], F32, "gated%d" % m, tag=tag)
+            nc.vector.scalar_tensor_tensor(gated[:], th[:], 1.0, yc[:], ALU.add, ALU.mult)
+            return gated
+
+        def statistics(m, gated, yb, tag=None):
+            lone[m] = tile([P, S + 1], F32, "lone%d" % m, tag=tag)
+            nc.gpsimd.tensor_scalar(lone[m][:, S : S + 1], minus_half[:], -2.0 * (0.4 * S) ** 0.5, 0.0, ALU.mult, ALU.add)
+            nc.vector.scalar_tensor_tensor(lone[m][:, :S], gated[:], 2.0, yb[:], ALU.add, ALU.mult)
+            squares = tile([P, S + 1], F32, "squares%d" % m)
+            total = tile([P, 1], F32, "total%d" % m)
+            nc.scalar.activation(squares[:], lone[m][:], ACT.Square, scale=S**-0.5, accum_out=total[:])
+            rstd = tile([P, 1], F32, "rstd%d" % m)
+            nc.gpsimd.tensor_tensor(rstd[:], total[:], minus_half[:], ALU.pow)
+            return rstd
+
+        def finish(m, rstd, pieces):
+            res = tile([P, S], F32, "res%d" % m)
+            for h in range(pieces):
+                cols = slice(h * S // pieces, (h + 1) * S // pieces)
+                nc.vector.scalar_tensor_tensor(res[:, cols], lone[m][:, cols], rstd[:], imp_sb[:, cols], ALU.mult, ALU.mult)
                 nc.sync.dma_start(out[m * P : (m + 1) * P, cols], res[:, cols])
+
+        cast("g", 0, on_s, on_s)
+        quantized_g0 = quantize(grouped["g", 0][:], PASSES * P, "g0")
+        picked.append(tile([P, S], U32, "picked1", tag="grouped_g0"))
+        nc.vector.tensor_copy(picked[1][:], word_table[1][:].bitcast(U32).indirect(offsets[:]))
+        yg0 = both_passes("g", 0, *quantized_g0)
+        cast("c", 0, on_s, on_s)
+        yc0 = product("c", 0)
+        cast("g", 1, on_s, on_v)
+        th0 = gate(raw["g", 1, 0], yg0)
+        yg1 = product("g", 1)
+        gated0 = cross(0, th0, yc0, "grouped_g1")
+        cast("c", 1, on_s, on_s)
+        th1 = gate(raw["c", 1, 1], yg1)
+        yc1 = product("c", 1)
+        cast("b", 0, on_v, on_v)
+        yb0 = product("b", 0)
+        cast("b", 1, on_s, on_s)
+        gated1 = cross(1, th1, yc1, "grouped_b0")
+        yb1 = psum.tile([P, S], F32, name="y_b1")
+        for o in range(PASSES):
+            codes, scales = quantize(grouped["b", 1][:, o * K_PASS : (o + 1) * K_PASS], P, "b1%d" % o)
+            mx_pass(yb1, codes[:], scales[:], o)
+        rstd0 = statistics(0, gated0, yb0, "grouped_b1")
+        rstd1 = statistics(1, gated1, yb1)
+        finish(0, rstd0, 1)
+        finish(1, rstd1, 2)

from contextlib import ExitStack

import concourse.mybir as mybir

K, T, S, N = 1024, 1024, 512, 256
P = 128
PACK = 4
K_PASS = P * PACK
PASSES = K // K_PASS
HALF = S // 2
FLOPS = 3 * 2 * K * N * S

F32 = mybir.dt.float32
BF16 = mybir.dt.bfloat16
I32 = mybir.dt.int32
U32 = mybir.dt.uint32
U16 = mybir.dt.uint16
U8 = mybir.dt.uint8
FP8X4 = mybir.dt.float8_e4m3fn_x4
ACT = mybir.ActivationFunctionType
ALU = mybir.AluOpType


def tile_picked_ygatcr_rms_p_kernel(tc, x_words, x_scales, w1, w2, w3, imp, offs, out):
    nc = tc.nc
    with ExitStack() as ctx:
        keep = ctx.enter_context(tc.tile_pool(name="keep", bufs=1))
        psum = ctx.enter_context(tc.psum_pool(name="psum", bufs=1))

        def tile(shape, dtype, name, tag=None):
            return keep.tile(shape, dtype, name=name, tag=tag or name, align_bytes=64)

        offsets = keep.tile([P, S // 16], U16, name="offsets")
        scale_table = tile([P, T], U8, "scale_table")
        nc.gpsimd.memset(scale_table[:].bitcast(I32), 0)
        minus_half = tile([P, 1], F32, "minus_half")
        nc.gpsimd.memset(minus_half[:], -0.5)
        lone = {}

        word_table = [tile([P, T], I32, "word_table%d" % o) for o in range(PASSES)]

        def load_x(o):
            nc.sync.dma_start(word_table[o][:], x_words[o].rearrange("p c r -> p (c r)").bitcast(I32))

        raw = {}

        def load_w(name, w, m, passes=range(PASSES)):
            for o in passes:
                raw[name, m, o] = tile([P, K_PASS], F32, "raw_%s%d%d" % (name, m, o))
                rows = w[o * K_PASS : (o + 1) * K_PASS, m * P : (m + 1) * P]
                nc.sync.dma_start(
                    raw[name, m, o][:].rearrange("p (t m) -> p t m", t=PACK),
                    rows.rearrange("(p t) m -> p t m", t=PACK),
                )

        load_w("g", w3, 0, [0])
        nc.sync.dma_start(offsets[:], offs)
        for q in range(4):
            nc.sync.dma_start(
                scale_table[32 * q : 32 * q + 8, :].bitcast(I32),
                x_scales[:, 4 * q : 4 * q + 4, :].bitcast(I32),
            )
        load_x(0)
        load_w("g", w3, 0, [1])
        load_x(1)
        load_w("c", w2, 0)
        load_w("g", w3, 1)
        load_w("c", w2, 1)
        load_w("b", w1, 0)
        load_w("b", w1, 1)
        imp_sb = tile([P, S], F32, "imp_sb")
        nc.sync.dma_start(imp_sb[:], imp)

        picked_scales = tile([P, S], U8, "picked_scales")
        picked = [tile([P, S], U32, "picked0")]
        nc.vector.tensor_copy(picked_scales[:], scale_table[:].indirect(offsets[:]))
        nc.vector.tensor_copy(picked[0][:], word_table[0][:].bitcast(U32).indirect(offsets[:]))

        def interleave(copy, dst, src):
            copy(dst.rearrange("p (c i t) -> p c t i", i=4, t=PACK), src.rearrange("p (t c i) -> p c t i", i=4, t=PACK))

        def quantize(grouped, width, name):
            codes = tile([P, width], U32, "codes_" + name)
            scales = tile([P, width], U8, "scales_" + name)
            nc.vector.quantize_mx(out=codes[:].bitcast(FP8X4), scales=scales[:], in_=grouped)
            return codes, scales

        def mx_pass(bank, codes, scales, o):
            nc.tensor.matmul_mx(
                out=bank[:],
                lhsT=codes.bitcast(FP8X4),
                lhsT_scale=scales,
                rhs=picked[o][:].bitcast(FP8X4),
                rhs_scale=picked_scales[4 * o : P, :],
                start=(o == 0),
                stop=(o == PASSES - 1),
            )

        on_v, on_s = nc.vector.tensor_copy, nc.scalar.copy
        grouped = {}

        def cast(name, m, first_copy, second_copy):
            grouped[name, m] = tile([P, PASSES * K_PASS], BF16, "grouped_%s%d" % (name, m))
            interleave(first_copy, grouped[name, m][:, :K_PASS], raw[name, m, 0][:])
            interleave(second_copy, grouped[name, m][:, K_PASS:], raw[name, m, 1][:])

        def both_passes(name, m, codes, scales):
            bank = psum.tile([P, S], F32, name="y_%s%d" % (name, m))
            for o in range(PASSES):
                mx_pass(bank, codes[:, o * P : (o + 1) * P], scales[:, o * P : (o + 1) * P], o)
            return bank

        def product(name, m):
            return both_passes(name, m, *quantize(grouped[name, m][:], PASSES * P, "%s%d" % (name, m)))

        def gate(th, yg):
            nc.scalar.activation(th[:], yg[:], ACT.Tanh, scale=0.5)
            return th

        def cross(m, th, yc, tag=None):
            gated = tile([P, S], F32, "gated%d" % m, tag=tag)
            nc.vector.scalar_tensor_tensor(gated[:], th[:], 1.0, yc[:], ALU.add, ALU.mult)
            return gated

        def statistics(m, gated, yb, tag=None):
            lone[m] = tile([P, S + 1], F32, "lone%d" % m, tag=tag)
            nc.gpsimd.tensor_scalar(lone[m][:, S : S + 1], minus_half[:], -2.0 * (0.4 * S) ** 0.5, 0.0, ALU.mult, ALU.add)
            nc.vector.scalar_tensor_tensor(lone[m][:, :S], gated[:], 2.0, yb[:], ALU.add, ALU.mult)
            squares = tile([P, S + 1], F32, "squares%d" % m)
            total = tile([P, 1], F32, "total%d" % m)
            nc.scalar.activation(squares[:], lone[m][:], ACT.Square, scale=S**-0.5, accum_out=total[:])
            rstd = tile([P, 1], F32, "rstd%d" % m)
            nc.gpsimd.tensor_tensor(rstd[:], total[:], minus_half[:], ALU.pow)
            return rstd

        def finish(m, rstd, pieces):
            res = tile([P, S], F32, "res%d" % m)
            for h in range(pieces):
                cols = slice(h * S // pieces, (h + 1) * S // pieces)
                nc.vector.scalar_tensor_tensor(res[:, cols], lone[m][:, cols], rstd[:], imp_sb[:, cols], ALU.mult, ALU.mult)
                nc.sync.dma_start(out[m * P : (m + 1) * P, cols], res[:, cols])

        cast("g", 0, on_s, on_s)
        quantized_g0 = quantize(grouped["g", 0][:], PASSES * P, "g0")
        picked.append(tile([P, S], U32, "picked1", tag="grouped_g0"))
        nc.vector.tensor_copy(picked[1][:], word_table[1][:].bitcast(U32).indirect(offsets[:]))
        yg0 = both_passes("g", 0, *quantized_g0)
        cast("c", 0, on_s, on_s)
        yc0 = product("c", 0)
        cast("g", 1, on_s, on_v)
        th0 = gate(raw["g", 1, 0], yg0)
        yg1 = product("g", 1)
        gated0 = cross(0, th0, yc0, "grouped_g1")
        cast("c", 1, on_s, on_s)
        th1 = gate(raw["c", 1, 1], yg1)
        yc1 = product("c", 1)
        cast("b", 0, on_v, on_v)
        yb0 = product("b", 0)
        cast("b", 1, on_s, on_s)
        gated1 = cross(1, th1, yc1, "grouped_b0")
        yb1 = psum.tile([P, S], F32, name="y_b1")
        for o in range(PASSES):
            codes, scales = quantize(grouped["b", 1][:, o * K_PASS : (o + 1) * K_PASS], P, "b1%d" % o)
            mx_pass(yb1, codes[:], scales[:], o)
        rstd0 = statistics(0, gated0, yb0, "grouped_b1")
        rstd1 = statistics(1, gated1, yb1)
        finish(0, rstd0, 1)
        finish(1, rstd1, 2)
